import numpy as np
import ml_dtypes

BF16 = ml_dtypes.bfloat16


def bf(x):
    return np.asarray(x, np.float32).astype(BF16)


def f32(x):
    return np.asarray(x, np.float32)


def f64(x):
    return np.asarray(x).astype(np.float64)


def striped(idx):
    return np.tile(idx.reshape(-1, 16).T, (8, 1))


S, K, M, N, D, V = 4096, 128, 128, 4096, 4, 1024


def setup_inputs():
    return {"table": bf(np.random.standard_normal((S, K))), "w": bf(np.random.standard_normal((D, K, M)) / np.sqrt(D * K)), "b": f32(0.5 * np.random.standard_normal((M, 1))), "offs": striped(np.random.permutation(np.tile(np.arange(S), 2))[:N])}


def reference(table, w, b, offs):
    idx = offs[:16].T.reshape(-1)
    x = f64(table)[idx].T
    y = sum(f64(w)[t].T @ x[:, t * V : (t + 1) * V] for t in range(D))
    return y + f64(b)

@@ -1,0 +1,68 @@
+import concourse.mybir as mybir
+from concourse.masks import make_identity
+
+BF16, F32, U16 = mybir.dt.bfloat16, mybir.dt.float32, mybir.dt.uint16
+
+P = 128
+NODES = 4096
+RELATIONS = 4
+OUT_COLS = 1024
+LIST = RELATIONS * OUT_COLS
+PIECE = 512
+BLOCKS = NODES // P
+BLOCKS_A_LOAD = 8
+BLOCKS_A_BANK = 4
+
+FLOPS = 2 * P * P * LIST
+
+
+def tile_gather_matmul_kernel(tc, table, w, b, offs, out):
+    nc = tc.nc
+    with (
+        tc.tile_pool(name="held", bufs=1) as held,
+        tc.tile_pool(name="results", bufs=2) as results,
+        tc.psum_pool(name="flips", bufs=4) as flips,
+        tc.psum_pool(name="sums", bufs=1) as sums,
+    ):
+        offsets = held.tile([P, LIST // 16], U16, name="offsets")
+        nc.sync.dma_start(offsets[:], offs)
+
+        by_load = table.rearrange("(c a p) k -> c p a k", a=BLOCKS_A_LOAD, p=P)
+        loads = []
+        for c in range(BLOCKS // BLOCKS_A_LOAD):
+            rows = held.tile([P, BLOCKS_A_LOAD, P], BF16, name="rows%d" % c)
+            queue = nc.sync if c % 2 == 0 else nc.scalar
+            queue.dma_start(rows[:], by_load[c])
+            loads.append(rows)
+
+        identity = held.tile([P, P], BF16, name="identity")
+        make_identity(nc, identity[:])
+
+        weights = held.tile([P, RELATIONS, P], BF16, name="weights")
+        nc.gpsimd.dma_start(weights[:], w.rearrange("t k m -> k t m"))
+        bias = held.tile([P, 1], F32, name="bias")
+        nc.gpsimd.dma_start(bias[:], b)
+
+        nodes = held.tile([P, NODES], BF16, name="nodes")
+        for g in range(BLOCKS // BLOCKS_A_BANK):
+            flipped = flips.tile([P, BLOCKS_A_BANK * P], BF16, name="flipped")
+            for i in range(BLOCKS_A_BANK):
+                c, a = divmod(g * BLOCKS_A_BANK + i, BLOCKS_A_LOAD)
+                nc.tensor.transpose(flipped[:, i * P : (i + 1) * P], loads[c][:, a, :], identity[:])
+            columns = nodes[:, g * BLOCKS_A_BANK * P : (g + 1) * BLOCKS_A_BANK * P]
+            if g % 2 == 0:
+                nc.vector.tensor_copy(columns, flipped[:])
+            else:
+                nc.scalar.copy(columns, flipped[:])
+
+        for h in range(OUT_COLS // PIECE):
+            total = sums.tile([P, PIECE], F32, name="total%d" % h)
+            for t in range(RELATIONS):
+                first = (t * OUT_COLS + h * PIECE) // 16
+                picked = nodes[:].indirect(offsets[:, first : first + PIECE // 16])
+                nc.tensor.matmul(
+                    total[:], weights[:, t, :], picked, start=(t == 0), stop=(t == RELATIONS - 1)
+                )
+            result = results.tile([P, PIECE], F32, name="result")
+            nc.vector.tensor_scalar_add(result[:], total[:], bias[:, 0:1])
+            nc.sync.dma_start(out[:, h * PIECE : (h + 1) * PIECE], result[:])

@@ -9,9 +9,9 @@ RELATIONS = 4
 OUT_COLS = 1024
 LIST = RELATIONS * OUT_COLS
 PIECE = 512
-BLOCKS = NODES // P
-BLOCKS_A_LOAD = 8
-BLOCKS_A_BANK = 4
+ROWS_A_PARTITION = 4
+GROUP = ROWS_A_PARTITION * P
+STORE = 256
 
 FLOPS = 2 * P * P * LIST
 
@@ -20,41 +20,41 @@ def tile_gather_matmul_kernel(tc, table, w, b, offs, out):
     nc = tc.nc
     with (
         tc.tile_pool(name="held", bufs=1) as held,
-        tc.tile_pool(name="results", bufs=2) as results,
         tc.psum_pool(name="flips", bufs=4) as flips,
         tc.psum_pool(name="sums", bufs=1) as sums,
     ):
-        offsets = held.tile([P, LIST // 16], U16, name="offsets")
-        nc.sync.dma_start(offsets[:], offs)
-
-        by_load = table.rearrange("(c a p) k -> c p a k", a=BLOCKS_A_LOAD, p=P)
-        loads = []
-        for c in range(BLOCKS // BLOCKS_A_LOAD):
-            rows = held.tile([P, BLOCKS_A_LOAD, P], BF16, name="rows%d" % c)
-            queue = nc.sync if c % 2 == 0 else nc.scalar
-            queue.dma_start(rows[:], by_load[c])
-            loads.append(rows)
-
         identity = held.tile([P, P], BF16, name="identity")
         make_identity(nc, identity[:])
 
+        by_group = table.rearrange("(g p j) k -> g p j k", p=P, j=ROWS_A_PARTITION)
+        loads = []
+        for g in range(NODES // GROUP):
+            rows = held.tile([P, ROWS_A_PARTITION, P], BF16, name="rows%d" % g)
+            nc.sync.dma_start(rows[:], by_group[g])
+            loads.append(rows)
+
+        offsets = held.tile([P, LIST // 16], U16, name="offsets")
+        nc.sync.dma_start(offsets[:], offs)
         weights = held.tile([P, RELATIONS, P], BF16, name="weights")
-        nc.gpsimd.dma_start(weights[:], w.rearrange("t k m -> k t m"))
+        nc.sync.dma_start(weights[:], w.rearrange("t k m -> k t m"))
         bias = held.tile([P, 1], F32, name="bias")
-        nc.gpsimd.dma_start(bias[:], b)
+        nc.sync.dma_start(bias[:], b)
 
         nodes = held.tile([P, NODES], BF16, name="nodes")
-        for g in range(BLOCKS // BLOCKS_A_BANK):
-            flipped = flips.tile([P, BLOCKS_A_BANK * P], BF16, name="flipped")
-            for i in range(BLOCKS_A_BANK):
-                c, a = divmod(g * BLOCKS_A_BANK + i, BLOCKS_A_LOAD)
-                nc.tensor.transpose(flipped[:, i * P : (i + 1) * P], loads[c][:, a, :], identity[:])
-            columns = nodes[:, g * BLOCKS_A_BANK * P : (g + 1) * BLOCKS_A_BANK * P]
-            if g % 2 == 0:
-                nc.vector.tensor_copy(columns, flipped[:])
+        for g in range(NODES // GROUP):
+            flipped = flips.tile([P, ROWS_A_PARTITION, P], BF16, name="flipped")
+            for j in range(ROWS_A_PARTITION):
+                nc.tensor.transpose(flipped[:, j, :], loads[g][:, j, :], identity[:])
+            columns = nodes[:, g * GROUP : (g + 1) * GROUP].rearrange(
+                "k (p j) -> k p j", j=ROWS_A_PARTITION
+            )
+            in_order = flipped[:].rearrange("k j p -> k p j")
+            if g % 2 == 1:
+                nc.vector.tensor_copy(columns, in_order)
             else:
-                nc.scalar.copy(columns, flipped[:])
+                nc.scalar.copy(columns, in_order)
 
+        result = held.tile([P, OUT_COLS], F32, name="result")
         for h in range(OUT_COLS // PIECE):
             total = sums.tile([P, PIECE], F32, name="total%d" % h)
             for t in range(RELATIONS):
@@ -63,6 +63,10 @@ def tile_gather_matmul_kernel(tc, table, w, b, offs, out):
                 nc.tensor.matmul(
                     total[:], weights[:, t, :], picked, start=(t == 0), stop=(t == RELATIONS - 1)
                 )
-            result = results.tile([P, PIECE], F32, name="result")
-            nc.vector.tensor_scalar_add(result[:], total[:], bias[:, 0:1])
-            nc.sync.dma_start(out[:, h * PIECE : (h + 1) * PIECE], result[:])
+            for s in range(PIECE // STORE):
+                lo = h * PIECE + s * STORE
+                nc.vector.tensor_scalar_add(
+                    result[:, lo : lo + STORE], total[:, s * STORE : (s + 1) * STORE], bias[:, 0:1]
+                )
+                queue = nc.sync if s == 0 else nc.scalar
+                queue.dma_start(out[:, lo : lo + STORE], result[:, lo : lo + STORE])

@@ -35,10 +35,11 @@ def tile_gather_matmul_kernel(tc, table, w, b, offs, out):
 
         offsets = held.tile([P, LIST // 16], U16, name="offsets")
         nc.sync.dma_start(offsets[:], offs)
+
         weights = held.tile([P, RELATIONS, P], BF16, name="weights")
-        nc.sync.dma_start(weights[:], w.rearrange("t k m -> k t m"))
+        nc.scalar.dma_start(weights[:], w.rearrange("t k m -> k t m"))
         bias = held.tile([P, 1], F32, name="bias")
-        nc.sync.dma_start(bias[:], b)
+        nc.scalar.dma_start(bias[:], b)
 
         nodes = held.tile([P, NODES], BF16, name="nodes")
         for g in range(NODES // GROUP):
@@ -49,7 +50,7 @@ def tile_gather_matmul_kernel(tc, table, w, b, offs, out):
                 "k (p j) -> k p j", j=ROWS_A_PARTITION
             )
             in_order = flipped[:].rearrange("k j p -> k p j")
-            if g % 2 == 1:
+            if g % 2 == 0:
                 nc.vector.tensor_copy(columns, in_order)
             else:
                 nc.scalar.copy(columns, in_order)

@@ -12,6 +12,9 @@ PIECE = 512
 ROWS_A_PARTITION = 4
 GROUP = ROWS_A_PARTITION * P
 STORE = 256
+WARM_UP = 4
+KEEP_WARM = 256
+BRIDGE = 2
 
 FLOPS = 2 * P * P * LIST
 
@@ -25,6 +28,12 @@ def tile_gather_matmul_kernel(tc, table, w, b, offs, out):
     ):
         identity = held.tile([P, P], BF16, name="identity")
         make_identity(nc, identity[:])
+
+        zeros = held.tile([P, PIECE], BF16, name="zeros")
+        nc.vector.memset(zeros[:], 0.0)
+        unread = sums.tile([P, PIECE], F32, name="unread")
+        for i in range(WARM_UP):
+            nc.tensor.matmul(unread[:], zeros[:, 0:P], zeros[:], start=True, stop=True)
 
         by_group = table.rearrange("(g p j) k -> g p j k", p=P, j=ROWS_A_PARTITION)
         loads = []
@@ -46,6 +55,10 @@ def tile_gather_matmul_kernel(tc, table, w, b, offs, out):
             flipped = flips.tile([P, ROWS_A_PARTITION, P], BF16, name="flipped")
             for j in range(ROWS_A_PARTITION):
                 nc.tensor.transpose(flipped[:, j, :], loads[g][:, j, :], identity[:])
+            as_columns = loads[g][:].rearrange("p j k -> p (j k)")
+            nc.tensor.matmul(
+                unread[:, 0:KEEP_WARM], identity[:], as_columns[:, 0:KEEP_WARM], start=True, stop=True
+            )
             columns = nodes[:, g * GROUP : (g + 1) * GROUP].rearrange(
                 "k (p j) -> k p j", j=ROWS_A_PARTITION
             )
@@ -54,6 +67,9 @@ def tile_gather_matmul_kernel(tc, table, w, b, offs, out):
                 nc.vector.tensor_copy(columns, in_order)
             else:
                 nc.scalar.copy(columns, in_order)
+
+        for i in range(BRIDGE):
+            nc.tensor.matmul(unread[:], identity[:], as_columns, start=True, stop=True)
 
         result = held.tile([P, OUT_COLS], F32, name="result")
         for h in range(OUT_COLS // PIECE):

@@ -35,6 +35,14 @@ def tile_gather_matmul_kernel(tc, table, w, b, offs, out):
         for i in range(WARM_UP):
             nc.tensor.matmul(unread[:], zeros[:, 0:P], zeros[:], start=True, stop=True)
 
+        weights = held.tile([P, RELATIONS, P], BF16, name="weights")
+        nc.scalar.dma_start(weights[:], w.rearrange("t k m -> k t m"))
+        bias = held.tile([P, 1], F32, name="bias")
+        nc.scalar.dma_start(bias[:], b)
+
+        early = held.tile([P, 1], BF16, name="early")
+        nc.scalar.copy(early[:], zeros[:, 0:1])
+
         by_group = table.rearrange("(g p j) k -> g p j k", p=P, j=ROWS_A_PARTITION)
         loads = []
         for g in range(NODES // GROUP):
@@ -44,11 +52,6 @@ def tile_gather_matmul_kernel(tc, table, w, b, offs, out):
 
         offsets = held.tile([P, LIST // 16], U16, name="offsets")
         nc.sync.dma_start(offsets[:], offs)
-
-        weights = held.tile([P, RELATIONS, P], BF16, name="weights")
-        nc.scalar.dma_start(weights[:], w.rearrange("t k m -> k t m"))
-        bias = held.tile([P, 1], F32, name="bias")
-        nc.scalar.dma_start(bias[:], b)
 
         nodes = held.tile([P, NODES], BF16, name="nodes")
         for g in range(NODES // GROUP):

import concourse.mybir as mybir
from concourse.masks import make_identity

BF16, F32, U16 = mybir.dt.bfloat16, mybir.dt.float32, mybir.dt.uint16

P = 128
NODES = 4096
RELATIONS = 4
OUT_COLS = 1024
LIST = RELATIONS * OUT_COLS
PIECE = 512
ROWS_A_PARTITION = 4
GROUP = ROWS_A_PARTITION * P
STORE = 256
WARM_UP = 4
KEEP_WARM = 256
BRIDGE = 2

FLOPS = 2 * P * P * LIST


def tile_gather_matmul_kernel(tc, table, w, b, offs, out):
    nc = tc.nc
    with (
        tc.tile_pool(name="held", bufs=1) as held,
        tc.psum_pool(name="flips", bufs=4) as flips,
        tc.psum_pool(name="sums", bufs=1) as sums,
    ):
        identity = held.tile([P, P], BF16, name="identity")
        make_identity(nc, identity[:])

        zeros = held.tile([P, PIECE], BF16, name="zeros")
        nc.vector.memset(zeros[:], 0.0)
        unread = sums.tile([P, PIECE], F32, name="unread")
        for i in range(WARM_UP):
            nc.tensor.matmul(unread[:], zeros[:, 0:P], zeros[:], start=True, stop=True)

        weights = held.tile([P, RELATIONS, P], BF16, name="weights")
        nc.scalar.dma_start(weights[:], w.rearrange("t k m -> k t m"))
        bias = held.tile([P, 1], F32, name="bias")
        nc.scalar.dma_start(bias[:], b)

        early = held.tile([P, 1], BF16, name="early")
        nc.scalar.copy(early[:], zeros[:, 0:1])

        by_group = table.rearrange("(g p j) k -> g p j k", p=P, j=ROWS_A_PARTITION)
        loads = []
        for g in range(NODES // GROUP):
            rows = held.tile([P, ROWS_A_PARTITION, P], BF16, name="rows%d" % g)
            nc.sync.dma_start(rows[:], by_group[g])
            loads.append(rows)

        offsets = held.tile([P, LIST // 16], U16, name="offsets")
        nc.sync.dma_start(offsets[:], offs)

        nodes = held.tile([P, NODES], BF16, name="nodes")
        for g in range(NODES // GROUP):
            flipped = flips.tile([P, ROWS_A_PARTITION, P], BF16, name="flipped")
            for j in range(ROWS_A_PARTITION):
                nc.tensor.transpose(flipped[:, j, :], loads[g][:, j, :], identity[:])
            as_columns = loads[g][:].rearrange("p j k -> p (j k)")
            nc.tensor.matmul(
                unread[:, 0:KEEP_WARM], identity[:], as_columns[:, 0:KEEP_WARM], start=True, stop=True
            )
            columns = nodes[:, g * GROUP : (g + 1) * GROUP].rearrange(
                "k (p j) -> k p j", j=ROWS_A_PARTITION
            )
            in_order = flipped[:].rearrange("k j p -> k p j")
            if g % 2 == 0:
                nc.vector.tensor_copy(columns, in_order)
            else:
                nc.scalar.copy(columns, in_order)

        for i in range(BRIDGE):
            nc.tensor.matmul(unread[:], identity[:], as_columns, start=True, stop=True)

        result = held.tile([P, OUT_COLS], F32, name="result")
        for h in range(OUT_COLS // PIECE):
            total = sums.tile([P, PIECE], F32, name="total%d" % h)
            for t in range(RELATIONS):
                first = (t * OUT_COLS + h * PIECE) // 16
                picked = nodes[:].indirect(offsets[:, first : first + PIECE // 16])
                nc.tensor.matmul(
                    total[:], weights[:, t, :], picked, start=(t == 0), stop=(t == RELATIONS - 1)
                )
            for s in range(PIECE // STORE):
                lo = h * PIECE + s * STORE
                nc.vector.tensor_scalar_add(
                    result[:, lo : lo + STORE], total[:, s * STORE : (s + 1) * STORE], bias[:, 0:1]
                )
                queue = nc.sync if s == 0 else nc.scalar
                queue.dma_start(out[:, lo : lo + STORE], result[:, lo : lo + STORE])
